import numpy as np
CORES = [0,1,2,3,4,5,6,7]
N = 8
GROUPS = [[0,1,2,3],[4,5,6,7]]
def setup_inputs(rng):
    return {"x": rng.standard_normal((N, 128, 8), dtype=np.float32)}
def reference(x):
    y = np.empty((N, 128, 8), x.dtype)
    for g in GROUPS:
        s = x[g].sum(axis=0, dtype=np.float64).astype(x[g].dtype)
        for r in g:
            y[r] = s
    return {"y": y}

from concourse.bass import DstId, RemoteDMATransfer
from concourse.mybir import AluOpType

W = 8
SLOTS = 4

SCRATCH = {
    "mine": ("sbuf", [128, W], "float32"),
    "land": ("sbuf", [128, SLOTS * W], "float32"),
}
SEMAPHORES = ["loaded", "summed", "sent", "arrived"]


def rank_program(g, core, T, topo):
    rank = T.rank_of(core)
    if rank is None:
        return
    group = [grp for grp in T.tables["GROUPS"] if rank in grp][0]
    pos = group.index(rank)
    peers = [T.cores[r] for r in group if r != rank]
    engines = 16
    mask = 0xFFFF

    g.dma_start(T.mine[:], T.x[:]).then_inc(T.sem.loaded, 16)
    g.dma_start(T.y[:], T.x[:]).then_inc(T.sem.summed, 16)
    summed = 16

    g.wait_ge(T.sem.loaded, 16)
    block = T.land[:, pos * W:(pos + 1) * W]
    ids = []
    for p in peers:
        rid, pid, sengine = topo.addr(p)
        ids.append(DstId(rid=rid, pnc=pid))
    g.remote_dma_fused(
        [RemoteDMATransfer(dst_ids=ids, dma_engine_mask=mask, remote_sem=T.sem.arrived,
                           srcs=[T.mine[:]], dsts=[block] * len(peers), alu_op=0)],
        local_sem=T.sem.sent)

    g.wait_ge(T.sem.arrived, engines * len(peers))
    g.wait_ge(T.sem.summed, summed)
    nodes = [None if p == pos else T.land[:, p * W:(p + 1) * W] for p in range(len(group))]
    while len(nodes) > 1:
        nxt = []
        for i in range(0, len(nodes) - 1, 2):
            a, b = nodes[i], nodes[i + 1]
            if b is None:
                a, b = b, a
            out = T.y[:] if a is None else a
            g.dma_start(out, b, accum_op=AluOpType.add).then_inc(T.sem.summed, 16)
            summed += 16
            nxt.append(a)
        if len(nodes) % 2:
            nxt.append(nodes[-1])
        g.wait_ge(T.sem.summed, summed)
        nodes = nxt

    g.wait_ge(T.sem.sent, engines)
